import numpy as np
import ml_dtypes


def mxq(x, axis, fmt="e4m3"):
    dtype, down = {"e4m3": (ml_dtypes.float8_e4m3fn, 7), "e5m2": (ml_dtypes.float8_e5m2, 14)}[fmt]
    v = np.moveaxis(np.asarray(x, np.float32).astype(ml_dtypes.bfloat16).astype(np.float64), axis, -1)
    blocks = v.reshape(v.shape[:-1] + (-1, 32))
    amax = np.abs(blocks).max(-1, keepdims=True)
    byte = np.maximum(np.where(amax > 0, np.frexp(amax)[1] - 1 + 127, 0) - down, 1)
    scale = np.exp2(byte - 127.0)
    codes = (blocks / scale).astype(np.float32).astype(dtype).astype(np.float64)
    return np.moveaxis((codes * scale).reshape(v.shape), -1, axis)


WIDE = False


def mx_kscale(k):
    if not WIDE:
        return np.ones(k)
    levels = np.array([10, -10, 5, -5, 0])
    if k % 512:
        return np.exp2(np.random.permutation(np.resize(levels, k // 32))).repeat(32)
    a = np.empty((k // 512, 16))
    for p in range(k // 512):
        a[p, :8] = np.random.permutation(np.resize(levels, 8))
        for g in range(8):
            far = levels[np.abs(levels - a[p, g]) >= 10]
            a[p, g + 8] = far[np.random.randint(len(far))]
    return np.exp2(a.ravel()).repeat(32)


def f64(x):
    return np.asarray(x).astype(np.float64)


def striped(idx):
    return np.tile(idx.reshape(-1, 16).T, (8, 1)).astype(np.uint16)


def unstriped(offs):
    return offs[:16].T.reshape(-1).astype(np.int64)


def striped8(idx):
    return np.concatenate([x.reshape(-1, 16).T for x in idx]).astype(np.uint16)


def runs(offs, k):
    lists = np.stack([offs[16 * r : 16 * r + 16].T.reshape(-1) for r in range(8)]).astype(np.int64)
    return lists[np.arange(k) % 512 // 64]


def pack_weight(w):
    k, n = w.shape
    w = f64(np.asarray(w, np.float32).astype(ml_dtypes.bfloat16)).reshape(k // 32, 32, n)
    amax = np.abs(w).max(1)
    byte = np.clip(np.where(amax > 0, np.frexp(amax)[1] - 1 + 127 - 7, 1), 1, 254)
    scaled = (w * np.exp2(127.0 - byte)[:, None, :]).reshape(k, n).astype(np.float32)
    words = np.ascontiguousarray(scaled.reshape(k // 512, 128, 4, n).transpose(0, 1, 3, 2)).astype(ml_dtypes.float8_e4m3fn).view(np.uint8)
    return words, np.ascontiguousarray(byte.astype(np.uint8).reshape(k // 512, 16, n))


def unpack_weight(words, scales):
    g, p, n, _ = words.shape
    vals = np.ascontiguousarray(words).view(ml_dtypes.float8_e4m3fn).astype(np.float64) * np.repeat(np.exp2(scales.astype(np.float64) - 127.0), 8, axis=1)[..., None]
    return vals.transpose(0, 1, 3, 2).reshape(g * 512, n)


E2M1 = np.array([0.0, 0.5, 1.0, 1.5, 2.0, 3.0, 4.0, 6.0, -0.0, -0.5, -1.0, -1.5, -2.0, -3.0, -4.0, -6.0])


def pack_fp4(w):
    k, n = w.shape
    w = f64(np.asarray(w, np.float32).astype(ml_dtypes.bfloat16)).reshape(k // 32, 32, n)
    amax = np.abs(w).max(1)
    mant, ex = np.frexp(amax / 6.0)
    byte = np.clip(np.where(amax > 0, np.where(mant > 0.5, ex, ex - 1) + 127, 1), 1, 254)
    scaled = (w * np.exp2(127.0 - byte)[:, None, :]).reshape(k, n).astype(np.float32)
    c = np.ascontiguousarray(scaled.reshape(k // 512, 128, 4, n).transpose(0, 1, 3, 2)).astype(ml_dtypes.float4_e2m1fn).view(np.uint8) & 0xF
    words = (c[..., 0::2] | (c[..., 1::2] << 4)).reshape(k // 512, 128, 2 * n)
    return np.ascontiguousarray(words), np.ascontiguousarray(byte.astype(np.uint8).reshape(k // 512, 16, n))


def unpack_fp4(words, scales):
    g, _, n = scales.shape
    words = np.ascontiguousarray(words).reshape(g, 128, n, 2)
    nib = np.empty((g, 128, n, 4), np.uint8)
    nib[..., 0::2] = words & 0xF
    nib[..., 1::2] = words >> 4
    vals = E2M1[nib] * np.repeat(np.exp2(scales.astype(np.float64) - 127.0), 8, axis=1)[..., None]
    return vals.transpose(0, 1, 3, 2).reshape(g * 512, n)


def planes(y):
    n, m = y.shape
    v = y.astype(np.float32).astype(ml_dtypes.bfloat16).astype(np.float64).reshape(n // 32, 32, m)
    top = np.abs(v).max(1)
    byte = np.clip(np.where(top > 0, np.frexp(top)[1] - 1 + 127 - 7, 1), 1, 254)
    codes = (v * np.exp2(127.0 - byte)[:, None, :]).reshape(n, m).astype(np.float32).astype(ml_dtypes.float8_e4m3fn).view(np.uint8)
    words = codes.reshape(n // 512, 128, 4, m).transpose(0, 1, 3, 2)
    return np.ascontiguousarray(words), np.ascontiguousarray(byte.astype(np.uint8).reshape(n // 512, 16, m))


K, T, S, V, N, H = 512, 2048, 512, 256, 512, 512


def setup_inputs():
    n = np.random.standard_normal
    s = mx_kscale(K)[:, None]
    u = mx_kscale(H)
    packed_xT = pack_weight(n((K, T)) * s)
    packed_w1 = pack_fp4(n((K, H)) / np.sqrt(K) / s)
    packed_w2 = pack_fp4(n((H, N)) / np.sqrt(H) / u[:, None])
    perm = np.stack([np.random.permutation(S) for _ in range(8)])
    return {
        "x_words": packed_xT[0],
        "x_scales": packed_xT[1],
        "w1_words": packed_w1[0],
        "w1_scales": packed_w1[1],
        "gn": (np.random.uniform(0.5, 1.5, (H, 1)) * u[:, None]).astype(np.float32),
        "w2_words": packed_w2[0],
        "w2_scales": packed_w2[1],
        "offs": striped(np.random.permutation(T)[:S]),
        "n1": striped8(np.stack([np.random.permutation(S) for _ in range(8)])),
        "la": striped8(perm[:, :V]),
        "lb": striped8(perm[:, V:]),
    }


def reference(x_words, x_scales, w1_words, w1_scales, gn, w2_words, w2_scales, offs, n1, la, lb):
    xq = unpack_weight(x_words, x_scales)[:, unstriped(offs)]
    y = unpack_fp4(w1_words, w1_scales).T @ xq
    a = y[np.arange(H)[:, None], runs(n1, H)]
    z = f64(gn) * ((y * a) / ((y) ** 2 + (a) ** 2 + 0.25))
    h = unpack_fp4(w2_words, w2_scales).T @ mxq(z, 0, "e4m3")
    c = h[np.arange(N)[:, None], runs(la, N)]
    d = h[np.arange(N)[:, None], runs(lb, N)]
    nb = np.minimum(c, d)
    na = np.maximum(c, d)
    p = np.zeros((N, S))
    p[np.arange(N)[:, None], runs(la, N)] = na
    out = p.copy()
    out[np.arange(N)[:, None], runs(lb, N)] = nb
    return (out,) + planes(out)

@@ -1,0 +1,225 @@
+from contextlib import ExitStack
+
+import concourse.mybir as mybir
+
+K, T, S, V, N, H = 512, 2048, 512, 256, 512, 512
+FLOPS = 2 * K * H * S + 2 * H * N * S
+
+F32 = mybir.dt.float32
+BF16 = mybir.dt.bfloat16
+I32 = mybir.dt.int32
+U32 = mybir.dt.uint32
+U16 = mybir.dt.uint16
+U8 = mybir.dt.uint8
+FP8X4 = mybir.dt.float8_e4m3fn_x4
+FP4X4 = mybir.dt.float4_e2m1fn_x4
+ALU = mybir.AluOpType
+ACT = mybir.ActivationFunctionType
+
+P = 128
+PACK = 4
+HALF = S // 2
+CHUNK = 128
+SPLIT = 352
+
+
+def load_scale_rows(queue, tile, rows):
+    for q in range(4):
+        queue.dma_start(out=tile[32 * q : 32 * q + 4, :].bitcast(I32), in_=rows[4 * q : 4 * q + 4, :].bitcast(I32))
+
+
+def deal_words(nc, words, raw):
+    nc.vector.tensor_copy(
+        out=words[:].rearrange("p (t m b) -> p t m b", t=PACK, b=2),
+        in_=raw[:].rearrange("p (m t b) -> p t m b", t=PACK, b=2),
+    )
+
+
+def deal_scales(nc, scales, raw):
+    nc.vector.tensor_copy(
+        out=scales[:].rearrange("p (t m) -> p t m", t=PACK),
+        in_=raw[:].rearrange("p (m t) -> p t m", t=PACK),
+    )
+
+
+def tile_picked_normord_none_po_kernel(
+    tc, x_words, x_scales, w1_words, w1_scales, gn, w2_words, w2_scales, offs, n1, la, lb, out_0, out_1, out_2
+):
+    nc = tc.nc
+    with ExitStack() as ctx:
+        lists = ctx.enter_context(tc.tile_pool(name="lists", bufs=1))
+        keep = ctx.enter_context(tc.tile_pool(name="keep", bufs=1))
+        psum = ctx.enter_context(tc.psum_pool(name="psum", bufs=8))
+
+        offs_sb = lists.tile([P, S // 16], U16, name="offs_sb")
+        n1_sb = lists.tile([P, S // 16], U16, name="n1_sb")
+        la_sb = lists.tile([P, V // 16], U16, name="la_sb")
+        lb_sb = lists.tile([P, V // 16], U16, name="lb_sb")
+
+        xw = keep.tile([P, T], U32, name="xw", align_bytes=64)
+        xs = keep.tile([P, T], U8, name="xs", align_bytes=64)
+        w1w_raw = keep.tile([P, 2 * H], U8, name="w1w_raw", align_bytes=64)
+        w1s_raw = keep.tile([P, H], U8, name="w1s_raw", align_bytes=64)
+        w2w_raw = keep.tile([P, 2 * N], U8, name="w2w_raw", align_bytes=64)
+        w2s_raw = keep.tile([P, N], U8, name="w2s_raw", align_bytes=64)
+        w1w = keep.tile([P, 2 * H], U8, name="w1w", align_bytes=64)
+        w2w = keep.tile([P, 2 * N], U8, name="w2w", align_bytes=64)
+        ws = keep.tile([P, H], U8, name="ws", align_bytes=64)
+        gain = keep.tile([P, PACK], F32, name="gain")
+        one = keep.tile([P, 1], F32, name="one")
+        warm = keep.tile([P, 1], F32, name="warm")
+
+        nc.vector.memset(w1s_raw[:].bitcast(I32), 0)
+        nc.vector.memset(one[:], 1.0)
+        nc.vector.memset(xs[:].bitcast(I32), 0)
+        nc.gpsimd.memset(w2s_raw[:].bitcast(I32), 0)
+
+        nc.scalar.dma_start(out=xw[:].bitcast(I32), in_=x_words[0].rearrange("p c r -> p (c r)").bitcast(I32))
+        nc.sync.dma_start(offs_sb[:], offs)
+        nc.sync.dma_start(out=w1w_raw[:].bitcast(I32), in_=w1_words[0].bitcast(I32))
+        load_scale_rows(nc.sync, w1s_raw, w1_scales[0])
+        nc.scalar.activation(out=warm[:], in_=one[:], func=ACT.Abs_reciprocal_sqrt)
+        load_scale_rows(nc.scalar, xs, x_scales[0])
+        nc.sync.dma_start(out=w2w_raw[:].bitcast(I32), in_=w2_words[0].bitcast(I32))
+        nc.sync.dma_start(n1_sb[:], n1)
+        nc.sync.dma_start(out=gain[:], in_=gn.rearrange("(p t) o -> p (t o)", t=PACK))
+        nc.sync.dma_start(la_sb[:], la)
+        nc.sync.dma_start(lb_sb[:], lb)
+        load_scale_rows(nc.gpsimd, w2s_raw, w2_scales[0])
+
+        deal_words(nc, w1w, w1w_raw)
+        deal_scales(nc, ws, w1s_raw)
+        deal_words(nc, w2w, w2w_raw)
+
+        xgw = [keep.tile([P, HALF], U32, name=f"xgw{u}", align_bytes=64) for u in range(2)]
+        xgs = [keep.tile([P, HALF], U8, name=f"xgs{u}", align_bytes=64) for u in range(2)]
+        y = [keep.tile([P, S], F32, name=f"y{t}") for t in range(PACK)]
+        halves = [slice(HALF * u, HALF * (u + 1)) for u in range(2)]
+        for u in range(2):
+            nc.vector.tensor_copy(out=xgw[u][:], in_=xw[:].indirect(offs_sb[:, 16 * u : 16 * u + 16]))
+            nc.vector.tensor_copy(out=xgs[u][:], in_=xs[:].indirect(offs_sb[:, 16 * u : 16 * u + 16]))
+            for t in range(PACK):
+                bank = psum.tile([P, S], F32, name="bank")
+                nc.tensor.matmul_mx(
+                    out=bank[:, 0:HALF],
+                    lhsT=w1w[:, 2 * P * t : 2 * P * (t + 1)].bitcast(FP4X4),
+                    lhsT_scale=ws[:, P * t : P * (t + 1)],
+                    rhs=xgw[u][:].bitcast(FP8X4),
+                    rhs_scale=xgs[u][:],
+                    start=True,
+                    stop=True,
+                )
+                nc.scalar.copy(out=y[t][:, halves[u]], in_=bank[:, 0:HALF])
+
+        a = keep.tile([P, PACK, S], F32, name="a")
+        aa = keep.tile([P, PACK, S], F32, name="aa")
+        yy = keep.tile([P, PACK, S], F32, name="yy")
+        hbank = [psum.tile([P, S], F32, name="bank") for t in range(PACK)]
+        h = [keep.tile([P, S], F32, name=f"h{t}") for t in range(PACK)]
+
+        for t in range(PACK):
+            for u in range(2):
+                nc.vector.tensor_copy(out=a[:, t, halves[u]], in_=y[t][:].indirect(n1_sb[:, 16 * u : 16 * u + 16]))
+        for t in range(PACK):
+            nc.scalar.activation(out=yy[:, t, :], in_=y[t][:], func=ACT.Square)
+        for u in range(2):
+            for t in range(PACK):
+                nc.scalar.activation(out=aa[:, t, halves[u]], in_=a[:, t, halves[u]], func=ACT.Square)
+        deal_scales(nc, ws, w2s_raw)
+
+        chunks = [slice(CHUNK * c, CHUNK * (c + 1)) for c in range(S // CHUNK)]
+        den = [keep.tile([P, PACK, CHUNK], F32, name=f"den{c}") for c in range(len(chunks))]
+        for c, cols in enumerate(chunks):
+            nc.vector.tensor_tensor(out=den[c][:], in0=aa[:, :, cols], in1=yy[:, :, cols], op=ALU.add)
+
+        last = S - CHUNK
+        for c, cols in enumerate(chunks):
+            root = keep.tile([P, PACK, CHUNK], F32, name=f"root{c}")
+            inv = keep.tile([P, PACK, CHUNK], F32, name=f"inv{c}")
+            scaled = keep.tile([P, PACK, CHUNK], F32, name=f"scaled{c}")
+            zb = keep.tile([P, CHUNK, PACK], BF16, name=f"zb{c}", align_bytes=64)
+            zw = keep.tile([P, CHUNK], U32, name=f"zw{c}", align_bytes=64)
+            zs = keep.tile([P, CHUNK], U8, name=f"zs{c}", align_bytes=64)
+            nc.scalar.activation(out=root[:], in_=den[c][:], func=ACT.Abs_reciprocal_sqrt, bias=0.25)
+            nc.scalar.activation(out=inv[:], in_=root[:], func=ACT.Square)
+            for t in range(PACK):
+                nc.vector.scalar_tensor_tensor(
+                    out=scaled[:, t, :], in0=y[t][:, cols], scalar=gain[:, t : t + 1], in1=inv[:, t, :],
+                    op0=ALU.mult, op1=ALU.mult,
+                )
+            nc.vector.tensor_tensor(
+                out=zb[:].rearrange("p (c i) t -> p c t i", i=4),
+                in0=scaled[:].rearrange("p t (c i) -> p c t i", i=4),
+                in1=a[:, :, cols].rearrange("p t (c i) -> p c t i", i=4),
+                op=ALU.mult,
+            )
+            nc.vector.quantize_mx(out=zw[:].bitcast(FP8X4), scales=zs[:], in_=zb[:].rearrange("p j t -> p (j t)"))
+            if c == len(chunks) - 1:
+                nc.scalar.copy(out=h[0][:, 0:last], in_=hbank[0][:, 0:last])
+            for t in range(PACK):
+                nc.tensor.matmul_mx(
+                    out=hbank[t][:, cols],
+                    lhsT=w2w[:, 2 * P * t : 2 * P * (t + 1)].bitcast(FP4X4),
+                    lhsT_scale=ws[:, P * t : P * (t + 1)],
+                    rhs=zw[:].bitcast(FP8X4),
+                    rhs_scale=zs[:],
+                    start=True,
+                    stop=True,
+                )
+        nc.scalar.copy(out=h[0][:, last:S], in_=hbank[0][:, last:S])
+        for t in range(1, PACK):
+            nc.scalar.copy(out=h[t][:], in_=hbank[t][:])
+
+        first = [keep.tile([P, V], F32, name=f"first{t}") for t in range(PACK)]
+        diff = [keep.tile([P, V], F32, name=f"diff{t}") for t in range(PACK)]
+        up = [keep.tile([P, V], F32, name=f"up{t}") for t in range(PACK)]
+        down = [keep.tile([P, V], F32, name=f"down{t}") for t in range(PACK)]
+        ndown = [keep.tile([P, V], F32, name=f"ndown{t}") for t in range(PACK)]
+        res = [keep.tile([P, S], F32, name=f"res{t}") for t in range(PACK)]
+        grouped = keep.tile([P, S, PACK], BF16, name="grouped", align_bytes=64)
+        out_rows = out_0.rearrange("(p t) j -> p t j", t=PACK)
+
+        for pair in range(2):
+            for t in (2 * pair, 2 * pair + 1):
+                nc.vector.tensor_copy(out=first[t][:], in_=h[t][:].indirect(la_sb[:]))
+            for t in (2 * pair, 2 * pair + 1):
+                nc.vector.tensor_tensor(out=diff[t][:], in0=h[t][:].indirect(lb_sb[:]), in1=first[t][:], op=ALU.subtract)
+                nc.scalar.activation(out=up[t][:], in_=diff[t][:], func=ACT.Relu)
+                nc.scalar.activation(out=ndown[t][:], in_=diff[t][:], func=ACT.Relu, scale=-1.0)
+                nc.scalar.activation(out=down[t][:], in_=ndown[t][:], func=ACT.Copy, scale=-1.0)
+
+        def put(t, places, step):
+            nc.vector.tensor_tensor(out=res[t][:].indirect(places[:]), in0=first[t][:], in1=step[t][:], op=ALU.add)
+
+        for pair in range(2):
+            for t in (2 * pair, 2 * pair + 1):
+                put(t, la_sb, up)
+            for t in (2 * pair, 2 * pair + 1):
+                put(t, lb_sb, down)
+                nc.sync.dma_start(out=out_rows[:, t, :], in_=res[t][:])
+                if t < 2:
+                    nc.scalar.copy(out=grouped[:, :, t], in_=res[t][:])
+                elif t == 2:
+                    nc.scalar.copy(
+                        out=grouped[:, 0:SPLIT, 2:4], in_=res[2][:, 0:SPLIT].unsqueeze(2).to_broadcast([P, SPLIT, 2])
+                    )
+                    nc.scalar.copy(out=grouped[:, SPLIT:S, 2], in_=res[2][:, SPLIT:S])
+
+        nc.vector.tensor_copy(out=grouped[:, 0:HALF, 3], in_=res[3][:, 0:HALF])
+        nc.scalar.copy(out=grouped[:, SPLIT:S, 3], in_=res[3][:, SPLIT:S])
+        nc.vector.tensor_copy(out=grouped[:, HALF:SPLIT, 3], in_=res[3][:, HALF:SPLIT])
+
+        ow = [keep.tile([P, HALF], U32, name=f"ow{u}", align_bytes=64) for u in range(2)]
+        osc = keep.tile([P, S], U8, name="osc", align_bytes=64)
+        words_out = out_1[0].rearrange("p c r -> p (c r)").bitcast(I32)
+        for u in range(2):
+            cols = slice(HALF * u, HALF * (u + 1))
+            nc.vector.quantize_mx(
+                out=ow[u][:].bitcast(FP8X4), scales=osc[:, cols], in_=grouped[:, cols, :].rearrange("p j t -> p (j t)")
+            )
+            nc.sync.dma_start(out=words_out[:, cols], in_=ow[u][:].bitcast(I32))
+        queues = [nc.scalar, nc.sync, nc.scalar, nc.sync]
+        for q in range(4):
+            queues[q].dma_start(
+                out=out_2[0, 4 * q : 4 * q + 4, :].bitcast(I32), in_=osc[32 * q : 32 * q + 4, :].bitcast(I32)
+            )

@@ -23,9 +23,9 @@ CHUNK = 128
 SPLIT = 352
 
 
-def load_scale_rows(queue, tile, rows):
+def load_scale_rows(queues, tile, rows):
     for q in range(4):
-        queue.dma_start(out=tile[32 * q : 32 * q + 4, :].bitcast(I32), in_=rows[4 * q : 4 * q + 4, :].bitcast(I32))
+        queues[q % len(queues)].dma_start(out=tile[32 * q : 32 * q + 4, :].bitcast(I32), in_=rows[4 * q : 4 * q + 4, :].bitcast(I32))
 
 
 def deal_words(nc, words, raw):
@@ -59,9 +59,8 @@ def tile_picked_normord_none_po_kernel(
         xw = keep.tile([P, T], U32, name="xw", align_bytes=64)
         xs = keep.tile([P, T], U8, name="xs", align_bytes=64)
         w1w_raw = keep.tile([P, 2 * H], U8, name="w1w_raw", align_bytes=64)
-        w1s_raw = keep.tile([P, H], U8, name="w1s_raw", align_bytes=64)
+        ws_raw = keep.tile([P, H], U8, name="ws_raw", align_bytes=64)
         w2w_raw = keep.tile([P, 2 * N], U8, name="w2w_raw", align_bytes=64)
-        w2s_raw = keep.tile([P, N], U8, name="w2s_raw", align_bytes=64)
         w1w = keep.tile([P, 2 * H], U8, name="w1w", align_bytes=64)
         w2w = keep.tile([P, 2 * N], U8, name="w2w", align_bytes=64)
         ws = keep.tile([P, H], U8, name="ws", align_bytes=64)
@@ -69,43 +68,43 @@ def tile_picked_normord_none_po_kernel(
         one = keep.tile([P, 1], F32, name="one")
         warm = keep.tile([P, 1], F32, name="warm")
 
-        nc.vector.memset(w1s_raw[:].bitcast(I32), 0)
-        nc.vector.memset(one[:], 1.0)
         nc.vector.memset(xs[:].bitcast(I32), 0)
-        nc.gpsimd.memset(w2s_raw[:].bitcast(I32), 0)
+        nc.vector.memset(ws_raw[:].bitcast(I32), 0)
+        nc.vector.memset(one[:], 1.0)
 
-        nc.scalar.dma_start(out=xw[:].bitcast(I32), in_=x_words[0].rearrange("p c r -> p (c r)").bitcast(I32))
         nc.sync.dma_start(offs_sb[:], offs)
         nc.sync.dma_start(out=w1w_raw[:].bitcast(I32), in_=w1_words[0].bitcast(I32))
-        load_scale_rows(nc.sync, w1s_raw, w1_scales[0])
-        nc.scalar.activation(out=warm[:], in_=one[:], func=ACT.Abs_reciprocal_sqrt)
-        load_scale_rows(nc.scalar, xs, x_scales[0])
         nc.sync.dma_start(out=w2w_raw[:].bitcast(I32), in_=w2_words[0].bitcast(I32))
+        load_scale_rows([nc.sync, nc.scalar], xs, x_scales[0])
+        nc.sync.dma_start(out=xw[:].bitcast(I32), in_=x_words[0].rearrange("p c r -> p (c r)").bitcast(I32))
+        nc.scalar.activation(out=warm[:], in_=one[:], func=ACT.Abs_reciprocal_sqrt)
+        load_scale_rows([nc.sync], ws_raw, w1_scales[0])
         nc.sync.dma_start(n1_sb[:], n1)
         nc.sync.dma_start(out=gain[:], in_=gn.rearrange("(p t) o -> p (t o)", t=PACK))
         nc.sync.dma_start(la_sb[:], la)
         nc.sync.dma_start(lb_sb[:], lb)
-        load_scale_rows(nc.gpsimd, w2s_raw, w2_scales[0])
-
-        deal_words(nc, w1w, w1w_raw)
-        deal_scales(nc, ws, w1s_raw)
-        deal_words(nc, w2w, w2w_raw)
 
         xgw = [keep.tile([P, HALF], U32, name=f"xgw{u}", align_bytes=64) for u in range(2)]
-        xgs = [keep.tile([P, HALF], U8, name=f"xgs{u}", align_bytes=64) for u in range(2)]
-        y = [keep.tile([P, S], F32, name=f"y{t}") for t in range(PACK)]
+        xgs = keep.tile([P, S], U8, name="xgs", align_bytes=64)
+        y = [keep.tile([P, 2 * S], F32, name=f"y{t}") for t in range(PACK)]
         halves = [slice(HALF * u, HALF * (u + 1)) for u in range(2)]
-        for u in range(2):
-            nc.vector.tensor_copy(out=xgw[u][:], in_=xw[:].indirect(offs_sb[:, 16 * u : 16 * u + 16]))
-            nc.vector.tensor_copy(out=xgs[u][:], in_=xs[:].indirect(offs_sb[:, 16 * u : 16 * u + 16]))
-            for t in range(PACK):
+
+        deal_words(nc, w1w, w1w_raw)
+        nc.vector.tensor_copy(out=xgs[:], in_=xs[:].indirect(offs_sb[:]))
+        deal_words(nc, w2w, w2w_raw)
+        nc.vector.tensor_copy(out=xgw[0][:], in_=xw[:].indirect(offs_sb[:, 0:16]))
+        deal_scales(nc, ws, ws_raw)
+        load_scale_rows([nc.sync], ws_raw, w2_scales[0])
+        nc.vector.tensor_copy(out=xgw[1][:], in_=xw[:].indirect(offs_sb[:, 16:32]))
+        for t in range(PACK):
+            for u in range(2):
                 bank = psum.tile([P, S], F32, name="bank")
                 nc.tensor.matmul_mx(
                     out=bank[:, 0:HALF],
                     lhsT=w1w[:, 2 * P * t : 2 * P * (t + 1)].bitcast(FP4X4),
                     lhsT_scale=ws[:, P * t : P * (t + 1)],
                     rhs=xgw[u][:].bitcast(FP8X4),
-                    rhs_scale=xgs[u][:],
+                    rhs_scale=xgs[:, halves[u]],
                     start=True,
                     stop=True,
                 )
@@ -115,50 +114,51 @@ def tile_picked_normord_none_po_kernel(
         aa = keep.tile([P, PACK, S], F32, name="aa")
         yy = keep.tile([P, PACK, S], F32, name="yy")
         hbank = [psum.tile([P, S], F32, name="bank") for t in range(PACK)]
+        hlast = [psum.tile([P, S], F32, name="bank") for t in range(PACK)]
         h = [keep.tile([P, S], F32, name=f"h{t}") for t in range(PACK)]
 
         for t in range(PACK):
-            for u in range(2):
-                nc.vector.tensor_copy(out=a[:, t, halves[u]], in_=y[t][:].indirect(n1_sb[:, 16 * u : 16 * u + 16]))
+            nc.vector.tensor_copy(out=a[:, t, :], in_=y[t][:].indirect(n1_sb[:]))
         for t in range(PACK):
-            nc.scalar.activation(out=yy[:, t, :], in_=y[t][:], func=ACT.Square)
+            nc.scalar.activation(out=yy[:, t, :], in_=y[t][:, 0:S], func=ACT.Square)
         for u in range(2):
             for t in range(PACK):
                 nc.scalar.activation(out=aa[:, t, halves[u]], in_=a[:, t, halves[u]], func=ACT.Square)
-        deal_scales(nc, ws, w2s_raw)
+        deal_scales(nc, ws, ws_raw)
 
         chunks = [slice(CHUNK * c, CHUNK * (c + 1)) for c in range(S // CHUNK)]
         den = [keep.tile([P, PACK, CHUNK], F32, name=f"den{c}") for c in range(len(chunks))]
         for c, cols in enumerate(chunks):
             nc.vector.tensor_tensor(out=den[c][:], in0=aa[:, :, cols], in1=yy[:, :, cols], op=ALU.add)
 
+        ya = yy
+        for u in range(2):
+            for t in range(PACK):
+                nc.vector.scalar_tensor_tensor(
+                    out=ya[:, t, halves[u]], in0=y[t][:, halves[u]], scalar=gain[:, t : t + 1], in1=a[:, t, halves[u]],
+                    op0=ALU.mult, op1=ALU.mult,
+                )
+
         last = S - CHUNK
         for c, cols in enumerate(chunks):
             root = keep.tile([P, PACK, CHUNK], F32, name=f"root{c}")
             inv = keep.tile([P, PACK, CHUNK], F32, name=f"inv{c}")
-            scaled = keep.tile([P, PACK, CHUNK], F32, name=f"scaled{c}")
             zb = keep.tile([P, CHUNK, PACK], BF16, name=f"zb{c}", align_bytes=64)
             zw = keep.tile([P, CHUNK], U32, name=f"zw{c}", align_bytes=64)
             zs = keep.tile([P, CHUNK], U8, name=f"zs{c}", align_bytes=64)
             nc.scalar.activation(out=root[:], in_=den[c][:], func=ACT.Abs_reciprocal_sqrt, bias=0.25)
             nc.scalar.activation(out=inv[:], in_=root[:], func=ACT.Square)
-            for t in range(PACK):
-                nc.vector.scalar_tensor_tensor(
-                    out=scaled[:, t, :], in0=y[t][:, cols], scalar=gain[:, t : t + 1], in1=inv[:, t, :],
-                    op0=ALU.mult, op1=ALU.mult,
-                )
             nc.vector.tensor_tensor(
                 out=zb[:].rearrange("p (c i) t -> p c t i", i=4),
-                in0=scaled[:].rearrange("p t (c i) -> p c t i", i=4),
-                in1=a[:, :, cols].rearrange("p t (c i) -> p c t i", i=4),
+                in0=ya[:, :, cols].rearrange("p t (c i) -> p c t i", i=4),
+                in1=inv[:].rearrange("p t (c i) -> p c t i", i=4),
                 op=ALU.mult,
             )
             nc.vector.quantize_mx(out=zw[:].bitcast(FP8X4), scales=zs[:], in_=zb[:].rearrange("p j t -> p (j t)"))
-            if c == len(chunks) - 1:
-                nc.scalar.copy(out=h[0][:, 0:last], in_=hbank[0][:, 0:last])
+            banks = hlast if c == len(chunks) - 1 else hbank
             for t in range(PACK):
                 nc.tensor.matmul_mx(
-                    out=hbank[t][:, cols],
+                    out=banks[t][:, cols],
                     lhsT=w2w[:, 2 * P * t : 2 * P * (t + 1)].bitcast(FP4X4),
                     lhsT_scale=ws[:, P * t : P * (t + 1)],
                     rhs=zw[:].bitcast(FP8X4),
@@ -166,9 +166,9 @@ def tile_picked_normord_none_po_kernel(
                     start=True,
                     stop=True,
                 )
-        nc.scalar.copy(out=h[0][:, last:S], in_=hbank[0][:, last:S])
-        for t in range(1, PACK):
-            nc.scalar.copy(out=h[t][:], in_=hbank[t][:])
+        for t in range(PACK):
+            nc.scalar.copy(out=h[t][:, 0:last], in_=hbank[t][:, 0:last])
+            nc.scalar.copy(out=h[t][:, last:S], in_=hlast[t][:, last:S])
 
         first = [keep.tile([P, V], F32, name=f"first{t}") for t in range(PACK)]
         diff = [keep.tile([P, V], F32, name=f"diff{t}") for t in range(PACK)]

@@ -35,10 +35,10 @@ def deal_words(nc, words, raw):
     )
 
 
-def deal_scales(nc, scales, raw):
+def deal_scales(nc, scales, raw, rows):
     nc.vector.tensor_copy(
-        out=scales[:].rearrange("p (t m) -> p t m", t=PACK),
-        in_=raw[:].rearrange("p (m t) -> p t m", t=PACK),
+        out=scales[:].rearrange("p (t m) -> p t m", t=PACK)[:, rows, :],
+        in_=raw[:].rearrange("p (m t) -> p t m", t=PACK)[:, rows, :],
     )
 
 
@@ -74,11 +74,13 @@ def tile_picked_normord_none_po_kernel(
 
         nc.sync.dma_start(offs_sb[:], offs)
         nc.sync.dma_start(out=w1w_raw[:].bitcast(I32), in_=w1_words[0].bitcast(I32))
-        nc.sync.dma_start(out=w2w_raw[:].bitcast(I32), in_=w2_words[0].bitcast(I32))
+        x_rows = x_words[0].rearrange("p c r -> p (c r)").bitcast(I32)
+        nc.sync.dma_start(out=xw[:, 0 : T // 2].bitcast(I32), in_=x_rows[:, 0 : T // 2])
         load_scale_rows([nc.sync, nc.scalar], xs, x_scales[0])
-        nc.sync.dma_start(out=xw[:].bitcast(I32), in_=x_words[0].rearrange("p c r -> p (c r)").bitcast(I32))
+        nc.sync.dma_start(out=xw[:, T // 2 : T].bitcast(I32), in_=x_rows[:, T // 2 : T])
         nc.scalar.activation(out=warm[:], in_=one[:], func=ACT.Abs_reciprocal_sqrt)
         load_scale_rows([nc.sync], ws_raw, w1_scales[0])
+        nc.sync.dma_start(out=w2w_raw[:].bitcast(I32), in_=w2_words[0].bitcast(I32))
         nc.sync.dma_start(n1_sb[:], n1)
         nc.sync.dma_start(out=gain[:], in_=gn.rearrange("(p t) o -> p (t o)", t=PACK))
         nc.sync.dma_start(la_sb[:], la)
@@ -91,11 +93,12 @@ def tile_picked_normord_none_po_kernel(
 
         deal_words(nc, w1w, w1w_raw)
         nc.vector.tensor_copy(out=xgs[:], in_=xs[:].indirect(offs_sb[:]))
-        deal_words(nc, w2w, w2w_raw)
         nc.vector.tensor_copy(out=xgw[0][:], in_=xw[:].indirect(offs_sb[:, 0:16]))
-        deal_scales(nc, ws, ws_raw)
+        deal_scales(nc, ws, ws_raw, slice(0, 1))
+        deal_scales(nc, ws, ws_raw, slice(1, PACK))
         load_scale_rows([nc.sync], ws_raw, w2_scales[0])
         nc.vector.tensor_copy(out=xgw[1][:], in_=xw[:].indirect(offs_sb[:, 16:32]))
+        deal_words(nc, w2w, w2w_raw)
         for t in range(PACK):
             for u in range(2):
                 bank = psum.tile([P, S], F32, name="bank")
@@ -112,7 +115,9 @@ def tile_picked_normord_none_po_kernel(
 
         a = keep.tile([P, PACK, S], F32, name="a")
         aa = keep.tile([P, PACK, S], F32, name="aa")
-        yy = keep.tile([P, PACK, S], F32, name="yy")
+        rows = keep.tile([P, PACK + 1, S], F32, name="rows")
+        yy = rows[:, 0:PACK, :]
+        ya = rows[:, 1 : PACK + 1, :]
         hbank = [psum.tile([P, S], F32, name="bank") for t in range(PACK)]
         hlast = [psum.tile([P, S], F32, name="bank") for t in range(PACK)]
         h = [keep.tile([P, S], F32, name=f"h{t}") for t in range(PACK)]
@@ -124,20 +129,23 @@ def tile_picked_normord_none_po_kernel(
         for u in range(2):
             for t in range(PACK):
                 nc.scalar.activation(out=aa[:, t, halves[u]], in_=a[:, t, halves[u]], func=ACT.Square)
-        deal_scales(nc, ws, ws_raw)
+        deal_scales(nc, ws, ws_raw, slice(0, PACK))
 
         chunks = [slice(CHUNK * c, CHUNK * (c + 1)) for c in range(S // CHUNK)]
         den = [keep.tile([P, PACK, CHUNK], F32, name=f"den{c}") for c in range(len(chunks))]
+
+        def product(t, cols):
+            nc.vector.scalar_tensor_tensor(
+                out=ya[:, t, cols], in0=y[t][:, cols], scalar=gain[:, t : t + 1], in1=a[:, t, cols],
+                op0=ALU.mult, op1=ALU.mult,
+            )
+
+        product(PACK - 1, slice(0, S))
         for c, cols in enumerate(chunks):
             nc.vector.tensor_tensor(out=den[c][:], in0=aa[:, :, cols], in1=yy[:, :, cols], op=ALU.add)
-
-        ya = yy
-        for u in range(2):
-            for t in range(PACK):
-                nc.vector.scalar_tensor_tensor(
-                    out=ya[:, t, halves[u]], in0=y[t][:, halves[u]], scalar=gain[:, t : t + 1], in1=a[:, t, halves[u]],
-                    op0=ALU.mult, op1=ALU.mult,
-                )
+        for cols in halves:
+            for t in range(PACK - 1):
+                product(t, cols)
 
         last = S - CHUNK
         for c, cols in enumerate(chunks):

@@ -74,13 +74,11 @@ def tile_picked_normord_none_po_kernel(
 
         nc.sync.dma_start(offs_sb[:], offs)
         nc.sync.dma_start(out=w1w_raw[:].bitcast(I32), in_=w1_words[0].bitcast(I32))
-        x_rows = x_words[0].rearrange("p c r -> p (c r)").bitcast(I32)
-        nc.sync.dma_start(out=xw[:, 0 : T // 2].bitcast(I32), in_=x_rows[:, 0 : T // 2])
+        nc.sync.dma_start(out=w2w_raw[:].bitcast(I32), in_=w2_words[0].bitcast(I32))
         load_scale_rows([nc.sync, nc.scalar], xs, x_scales[0])
-        nc.sync.dma_start(out=xw[:, T // 2 : T].bitcast(I32), in_=x_rows[:, T // 2 : T])
+        nc.sync.dma_start(out=xw[:].bitcast(I32), in_=x_words[0].rearrange("p c r -> p (c r)").bitcast(I32))
         nc.scalar.activation(out=warm[:], in_=one[:], func=ACT.Abs_reciprocal_sqrt)
         load_scale_rows([nc.sync], ws_raw, w1_scales[0])
-        nc.sync.dma_start(out=w2w_raw[:].bitcast(I32), in_=w2_words[0].bitcast(I32))
         nc.sync.dma_start(n1_sb[:], n1)
         nc.sync.dma_start(out=gain[:], in_=gn.rearrange("(p t) o -> p (t o)", t=PACK))
         nc.sync.dma_start(la_sb[:], la)
@@ -93,12 +91,12 @@ def tile_picked_normord_none_po_kernel(
 
         deal_words(nc, w1w, w1w_raw)
         nc.vector.tensor_copy(out=xgs[:], in_=xs[:].indirect(offs_sb[:]))
+        deal_words(nc, w2w, w2w_raw)
         nc.vector.tensor_copy(out=xgw[0][:], in_=xw[:].indirect(offs_sb[:, 0:16]))
         deal_scales(nc, ws, ws_raw, slice(0, 1))
         deal_scales(nc, ws, ws_raw, slice(1, PACK))
         load_scale_rows([nc.sync], ws_raw, w2_scales[0])
         nc.vector.tensor_copy(out=xgw[1][:], in_=xw[:].indirect(offs_sb[:, 16:32]))
-        deal_words(nc, w2w, w2w_raw)
         for t in range(PACK):
             for u in range(2):
                 bank = psum.tile([P, S], F32, name="bank")

from contextlib import ExitStack

import concourse.mybir as mybir

K, T, S, V, N, H = 512, 2048, 512, 256, 512, 512
FLOPS = 2 * K * H * S + 2 * H * N * S

F32 = mybir.dt.float32
BF16 = mybir.dt.bfloat16
I32 = mybir.dt.int32
U32 = mybir.dt.uint32
U16 = mybir.dt.uint16
U8 = mybir.dt.uint8
FP8X4 = mybir.dt.float8_e4m3fn_x4
FP4X4 = mybir.dt.float4_e2m1fn_x4
ALU = mybir.AluOpType
ACT = mybir.ActivationFunctionType

P = 128
PACK = 4
HALF = S // 2
CHUNK = 128
SPLIT = 352


def load_scale_rows(queues, tile, rows):
    for q in range(4):
        queues[q % len(queues)].dma_start(out=tile[32 * q : 32 * q + 4, :].bitcast(I32), in_=rows[4 * q : 4 * q + 4, :].bitcast(I32))


def deal_words(nc, words, raw):
    nc.vector.tensor_copy(
        out=words[:].rearrange("p (t m b) -> p t m b", t=PACK, b=2),
        in_=raw[:].rearrange("p (m t b) -> p t m b", t=PACK, b=2),
    )


def deal_scales(nc, scales, raw, rows):
    nc.vector.tensor_copy(
        out=scales[:].rearrange("p (t m) -> p t m", t=PACK)[:, rows, :],
        in_=raw[:].rearrange("p (m t) -> p t m", t=PACK)[:, rows, :],
    )


def tile_picked_normord_none_po_kernel(
    tc, x_words, x_scales, w1_words, w1_scales, gn, w2_words, w2_scales, offs, n1, la, lb, out_0, out_1, out_2
):
    nc = tc.nc
    with ExitStack() as ctx:
        lists = ctx.enter_context(tc.tile_pool(name="lists", bufs=1))
        keep = ctx.enter_context(tc.tile_pool(name="keep", bufs=1))
        psum = ctx.enter_context(tc.psum_pool(name="psum", bufs=8))

        offs_sb = lists.tile([P, S // 16], U16, name="offs_sb")
        n1_sb = lists.tile([P, S // 16], U16, name="n1_sb")
        la_sb = lists.tile([P, V // 16], U16, name="la_sb")
        lb_sb = lists.tile([P, V // 16], U16, name="lb_sb")

        xw = keep.tile([P, T], U32, name="xw", align_bytes=64)
        xs = keep.tile([P, T], U8, name="xs", align_bytes=64)
        w1w_raw = keep.tile([P, 2 * H], U8, name="w1w_raw", align_bytes=64)
        ws_raw = keep.tile([P, H], U8, name="ws_raw", align_bytes=64)
        w2w_raw = keep.tile([P, 2 * N], U8, name="w2w_raw", align_bytes=64)
        w1w = keep.tile([P, 2 * H], U8, name="w1w", align_bytes=64)
        w2w = keep.tile([P, 2 * N], U8, name="w2w", align_bytes=64)
        ws = keep.tile([P, H], U8, name="ws", align_bytes=64)
        gain = keep.tile([P, PACK], F32, name="gain")
        one = keep.tile([P, 1], F32, name="one")
        warm = keep.tile([P, 1], F32, name="warm")

        nc.vector.memset(xs[:].bitcast(I32), 0)
        nc.vector.memset(ws_raw[:].bitcast(I32), 0)
        nc.vector.memset(one[:], 1.0)

        nc.sync.dma_start(offs_sb[:], offs)
        nc.sync.dma_start(out=w1w_raw[:].bitcast(I32), in_=w1_words[0].bitcast(I32))
        nc.sync.dma_start(out=w2w_raw[:].bitcast(I32), in_=w2_words[0].bitcast(I32))
        load_scale_rows([nc.sync, nc.scalar], xs, x_scales[0])
        nc.sync.dma_start(out=xw[:].bitcast(I32), in_=x_words[0].rearrange("p c r -> p (c r)").bitcast(I32))
        nc.scalar.activation(out=warm[:], in_=one[:], func=ACT.Abs_reciprocal_sqrt)
        load_scale_rows([nc.sync], ws_raw, w1_scales[0])
        nc.sync.dma_start(n1_sb[:], n1)
        nc.sync.dma_start(out=gain[:], in_=gn.rearrange("(p t) o -> p (t o)", t=PACK))
        nc.sync.dma_start(la_sb[:], la)
        nc.sync.dma_start(lb_sb[:], lb)

        xgw = [keep.tile([P, HALF], U32, name=f"xgw{u}", align_bytes=64) for u in range(2)]
        xgs = keep.tile([P, S], U8, name="xgs", align_bytes=64)
        y = [keep.tile([P, 2 * S], F32, name=f"y{t}") for t in range(PACK)]
        halves = [slice(HALF * u, HALF * (u + 1)) for u in range(2)]

        deal_words(nc, w1w, w1w_raw)
        nc.vector.tensor_copy(out=xgs[:], in_=xs[:].indirect(offs_sb[:]))
        deal_words(nc, w2w, w2w_raw)
        nc.vector.tensor_copy(out=xgw[0][:], in_=xw[:].indirect(offs_sb[:, 0:16]))
        deal_scales(nc, ws, ws_raw, slice(0, 1))
        deal_scales(nc, ws, ws_raw, slice(1, PACK))
        load_scale_rows([nc.sync], ws_raw, w2_scales[0])
        nc.vector.tensor_copy(out=xgw[1][:], in_=xw[:].indirect(offs_sb[:, 16:32]))
        for t in range(PACK):
            for u in range(2):
                bank = psum.tile([P, S], F32, name="bank")
                nc.tensor.matmul_mx(
                    out=bank[:, 0:HALF],
                    lhsT=w1w[:, 2 * P * t : 2 * P * (t + 1)].bitcast(FP4X4),
                    lhsT_scale=ws[:, P * t : P * (t + 1)],
                    rhs=xgw[u][:].bitcast(FP8X4),
                    rhs_scale=xgs[:, halves[u]],
                    start=True,
                    stop=True,
                )
                nc.scalar.copy(out=y[t][:, halves[u]], in_=bank[:, 0:HALF])

        a = keep.tile([P, PACK, S], F32, name="a")
        aa = keep.tile([P, PACK, S], F32, name="aa")
        rows = keep.tile([P, PACK + 1, S], F32, name="rows")
        yy = rows[:, 0:PACK, :]
        ya = rows[:, 1 : PACK + 1, :]
        hbank = [psum.tile([P, S], F32, name="bank") for t in range(PACK)]
        hlast = [psum.tile([P, S], F32, name="bank") for t in range(PACK)]
        h = [keep.tile([P, S], F32, name=f"h{t}") for t in range(PACK)]

        for t in range(PACK):
            nc.vector.tensor_copy(out=a[:, t, :], in_=y[t][:].indirect(n1_sb[:]))
        for t in range(PACK):
            nc.scalar.activation(out=yy[:, t, :], in_=y[t][:, 0:S], func=ACT.Square)
        for u in range(2):
            for t in range(PACK):
                nc.scalar.activation(out=aa[:, t, halves[u]], in_=a[:, t, halves[u]], func=ACT.Square)
        deal_scales(nc, ws, ws_raw, slice(0, PACK))

        chunks = [slice(CHUNK * c, CHUNK * (c + 1)) for c in range(S // CHUNK)]
        den = [keep.tile([P, PACK, CHUNK], F32, name=f"den{c}") for c in range(len(chunks))]

        def product(t, cols):
            nc.vector.scalar_tensor_tensor(
                out=ya[:, t, cols], in0=y[t][:, cols], scalar=gain[:, t : t + 1], in1=a[:, t, cols],
                op0=ALU.mult, op1=ALU.mult,
            )

        product(PACK - 1, slice(0, S))
        for c, cols in enumerate(chunks):
            nc.vector.tensor_tensor(out=den[c][:], in0=aa[:, :, cols], in1=yy[:, :, cols], op=ALU.add)
        for cols in halves:
            for t in range(PACK - 1):
                product(t, cols)

        last = S - CHUNK
        for c, cols in enumerate(chunks):
            root = keep.tile([P, PACK, CHUNK], F32, name=f"root{c}")
            inv = keep.tile([P, PACK, CHUNK], F32, name=f"inv{c}")
            zb = keep.tile([P, CHUNK, PACK], BF16, name=f"zb{c}", align_bytes=64)
            zw = keep.tile([P, CHUNK], U32, name=f"zw{c}", align_bytes=64)
            zs = keep.tile([P, CHUNK], U8, name=f"zs{c}", align_bytes=64)
            nc.scalar.activation(out=root[:], in_=den[c][:], func=ACT.Abs_reciprocal_sqrt, bias=0.25)
            nc.scalar.activation(out=inv[:], in_=root[:], func=ACT.Square)
            nc.vector.tensor_tensor(
                out=zb[:].rearrange("p (c i) t -> p c t i", i=4),
                in0=ya[:, :, cols].rearrange("p t (c i) -> p c t i", i=4),
                in1=inv[:].rearrange("p t (c i) -> p c t i", i=4),
                op=ALU.mult,
            )
            nc.vector.quantize_mx(out=zw[:].bitcast(FP8X4), scales=zs[:], in_=zb[:].rearrange("p j t -> p (j t)"))
            banks = hlast if c == len(chunks) - 1 else hbank
            for t in range(PACK):
                nc.tensor.matmul_mx(
                    out=banks[t][:, cols],
                    lhsT=w2w[:, 2 * P * t : 2 * P * (t + 1)].bitcast(FP4X4),
                    lhsT_scale=ws[:, P * t : P * (t + 1)],
                    rhs=zw[:].bitcast(FP8X4),
                    rhs_scale=zs[:],
                    start=True,
                    stop=True,
                )
        for t in range(PACK):
            nc.scalar.copy(out=h[t][:, 0:last], in_=hbank[t][:, 0:last])
            nc.scalar.copy(out=h[t][:, last:S], in_=hlast[t][:, last:S])

        first = [keep.tile([P, V], F32, name=f"first{t}") for t in range(PACK)]
        diff = [keep.tile([P, V], F32, name=f"diff{t}") for t in range(PACK)]
        up = [keep.tile([P, V], F32, name=f"up{t}") for t in range(PACK)]
        down = [keep.tile([P, V], F32, name=f"down{t}") for t in range(PACK)]
        ndown = [keep.tile([P, V], F32, name=f"ndown{t}") for t in range(PACK)]
        res = [keep.tile([P, S], F32, name=f"res{t}") for t in range(PACK)]
        grouped = keep.tile([P, S, PACK], BF16, name="grouped", align_bytes=64)
        out_rows = out_0.rearrange("(p t) j -> p t j", t=PACK)

        for pair in range(2):
            for t in (2 * pair, 2 * pair + 1):
                nc.vector.tensor_copy(out=first[t][:], in_=h[t][:].indirect(la_sb[:]))
            for t in (2 * pair, 2 * pair + 1):
                nc.vector.tensor_tensor(out=diff[t][:], in0=h[t][:].indirect(lb_sb[:]), in1=first[t][:], op=ALU.subtract)
                nc.scalar.activation(out=up[t][:], in_=diff[t][:], func=ACT.Relu)
                nc.scalar.activation(out=ndown[t][:], in_=diff[t][:], func=ACT.Relu, scale=-1.0)
                nc.scalar.activation(out=down[t][:], in_=ndown[t][:], func=ACT.Copy, scale=-1.0)

        def put(t, places, step):
            nc.vector.tensor_tensor(out=res[t][:].indirect(places[:]), in0=first[t][:], in1=step[t][:], op=ALU.add)

        for pair in range(2):
            for t in (2 * pair, 2 * pair + 1):
                put(t, la_sb, up)
            for t in (2 * pair, 2 * pair + 1):
                put(t, lb_sb, down)
                nc.sync.dma_start(out=out_rows[:, t, :], in_=res[t][:])
                if t < 2:
                    nc.scalar.copy(out=grouped[:, :, t], in_=res[t][:])
                elif t == 2:
                    nc.scalar.copy(
                        out=grouped[:, 0:SPLIT, 2:4], in_=res[2][:, 0:SPLIT].unsqueeze(2).to_broadcast([P, SPLIT, 2])
                    )
                    nc.scalar.copy(out=grouped[:, SPLIT:S, 2], in_=res[2][:, SPLIT:S])

        nc.vector.tensor_copy(out=grouped[:, 0:HALF, 3], in_=res[3][:, 0:HALF])
        nc.scalar.copy(out=grouped[:, SPLIT:S, 3], in_=res[3][:, SPLIT:S])
        nc.vector.tensor_copy(out=grouped[:, HALF:SPLIT, 3], in_=res[3][:, HALF:SPLIT])

        ow = [keep.tile([P, HALF], U32, name=f"ow{u}", align_bytes=64) for u in range(2)]
        osc = keep.tile([P, S], U8, name="osc", align_bytes=64)
        words_out = out_1[0].rearrange("p c r -> p (c r)").bitcast(I32)
        for u in range(2):
            cols = slice(HALF * u, HALF * (u + 1))
            nc.vector.quantize_mx(
                out=ow[u][:].bitcast(FP8X4), scales=osc[:, cols], in_=grouped[:, cols, :].rearrange("p j t -> p (j t)")
            )
            nc.sync.dma_start(out=words_out[:, cols], in_=ow[u][:].bitcast(I32))
        queues = [nc.scalar, nc.sync, nc.scalar, nc.sync]
        for q in range(4):
            queues[q].dma_start(
                out=out_2[0, 4 * q : 4 * q + 4, :].bitcast(I32), in_=osc[32 * q : 32 * q + 4, :].bitcast(I32)
            )
